import numpy as np
import ml_dtypes


def mxq(x, axis, fmt="e4m3"):
    dtype, down = {"e4m3": (ml_dtypes.float8_e4m3fn, 7), "e5m2": (ml_dtypes.float8_e5m2, 14)}[fmt]
    v = np.moveaxis(np.asarray(x, np.float32).astype(ml_dtypes.bfloat16).astype(np.float64), axis, -1)
    blocks = v.reshape(v.shape[:-1] + (-1, 32))
    amax = np.abs(blocks).max(-1, keepdims=True)
    byte = np.maximum(np.where(amax > 0, np.frexp(amax)[1] - 1 + 127, 0) - down, 1)
    scale = np.exp2(byte - 127.0)
    codes = (blocks / scale).astype(np.float32).astype(dtype).astype(np.float64)
    return np.moveaxis((codes * scale).reshape(v.shape), -1, axis)


WIDE = False


def mx_kscale(k):
    if not WIDE:
        return np.ones(k)
    levels = np.array([10, -10, 5, -5, 0])
    if k % 512:
        return np.exp2(np.random.permutation(np.resize(levels, k // 32))).repeat(32)
    a = np.empty((k // 512, 16))
    for p in range(k // 512):
        a[p, :8] = np.random.permutation(np.resize(levels, 8))
        for g in range(8):
            far = levels[np.abs(levels - a[p, g]) >= 10]
            a[p, g + 8] = far[np.random.randint(len(far))]
    return np.exp2(a.ravel()).repeat(32)


def f64(x):
    return np.asarray(x).astype(np.float64)


def striped(idx):
    return np.tile(idx.reshape(-1, 16).T, (8, 1)).astype(np.uint16)


def unstriped(offs):
    return offs[:16].T.reshape(-1).astype(np.int64)


def pack_weight(w):
    k, n = w.shape
    w = f64(np.asarray(w, np.float32).astype(ml_dtypes.bfloat16)).reshape(k // 32, 32, n)
    amax = np.abs(w).max(1)
    byte = np.clip(np.where(amax > 0, np.frexp(amax)[1] - 1 + 127 - 7, 1), 1, 254)
    scaled = (w * np.exp2(127.0 - byte)[:, None, :]).reshape(k, n).astype(np.float32)
    words = np.ascontiguousarray(scaled.reshape(k // 512, 128, 4, n).transpose(0, 1, 3, 2)).astype(ml_dtypes.float8_e4m3fn).view(np.uint8)
    return words, np.ascontiguousarray(byte.astype(np.uint8).reshape(k // 512, 16, n))


def unpack_weight(words, scales):
    g, p, n, _ = words.shape
    vals = np.ascontiguousarray(words).view(ml_dtypes.float8_e4m3fn).astype(np.float64) * np.repeat(np.exp2(scales.astype(np.float64) - 127.0), 8, axis=1)[..., None]
    return vals.transpose(0, 1, 3, 2).reshape(g * 512, n)


K, T, S, D, N, V = 512, 2048, 1024, 8, 256, 128
P = 2 ** 7


def setup_inputs():
    n = np.random.standard_normal
    s = mx_kscale(K)[:, None]
    packed_xT = pack_weight(n((K, T)) * s)
    return {
        "x_words": packed_xT[0],
        "x_scales": packed_xT[1],
        "w1": (n((K, N)) / np.sqrt(K) / s).astype(np.float32),
        "w2": (n((K, N)) / np.sqrt(K) / s).astype(np.float32),
        "alpha": (np.tile(np.random.uniform(0.65, 0.75, V) * D * D, (P, 1))).astype(np.float32),
        "offs": striped(np.random.permutation(T)[:S]),
        "oth": striped(np.random.permutation(S)),
    }


def reference(x_words, x_scales, w1, w2, alpha, offs, oth):
    xq = unpack_weight(x_words, x_scales)[:, unstriped(offs)]
    y = mxq(f64(w1), 0, "e4m3").T @ xq
    z = mxq(f64(w2), 0, "e4m3").T @ xq
    reg = np.maximum(np.log(np.exp(y) + 1.0), np.log(np.exp(z) + 1.0))
    inv = np.exp(-0.693147 * reg)
    tot = inv.reshape(len(inv), -1, D).sum(axis=2)
    uni = np.maximum(reg, reg[:, unstriped(oth)])
    iu = np.exp(-0.693147 * uni)
    tu = iu.reshape(len(iu), -1, D).sum(axis=2)
    est = f64(alpha)[:1] / tot
    return np.log(tot / tu) + 0.02 * est

@@ -1,0 +1,172 @@
+import math
+from contextlib import ExitStack
+
+import concourse.mybir as mybir
+from concourse.masks import make_identity
+
+F32 = mybir.dt.float32
+BF16 = mybir.dt.bfloat16
+I32 = mybir.dt.int32
+U32 = mybir.dt.uint32
+U16 = mybir.dt.uint16
+U8 = mybir.dt.uint8
+FP8X4 = mybir.dt.float8_e4m3fn_x4
+ALU = mybir.AluOpType
+ACT = mybir.ActivationFunctionType
+
+P = 128
+K, T, S, D, N, V = 512, 2048, 1024, 8, 256, 128
+HALF = 512
+PIECE = 256
+FLOPS = 2 * 2 * K * N * S
+RATE = 0.693147
+SHIFT_BITS = 64
+RATIO_BITS = 28
+
+
+def tile_picked_yhll_union_p_kernel(tc, x_words, x_scales, w1, w2, alpha, offs, oth, out):
+    nc = tc.nc
+    with ExitStack() as ctx:
+        keep = ctx.enter_context(tc.tile_pool(name="keep", bufs=1))
+        psum = ctx.enter_context(tc.psum_pool(name="psum", bufs=1))
+
+        offs_sb = keep.tile([P, S // 16], U16, name="offs_sb")
+        oth_sb = keep.tile([P, S // 16], U16, name="oth_sb")
+        xs_sb = keep.tile([P, T], U8, name="xs_sb", align_bytes=64)
+
+        def constant_column(name, value, slot):
+            unit = keep.tile([P, 1], F32, name=name + "_unit", tag=slot, align_bytes=64)
+            col = keep.tile([P, 1], F32, name=name)
+            nc.vector.memset(unit[:], 1.0)
+            nc.vector.tensor_scalar_mul(col[:], unit[:], value)
+            return col
+
+        nc.vector.memset(xs_sb[:].bitcast(I32), 0)
+        floor_col = constant_column("floor_col", 2.0 ** -SHIFT_BITS, "x_slot")
+        shift_col = constant_column("shift_col", -RATIO_BITS * math.log(2.0), "w1b_slot")
+        rate_col = constant_column("rate_col", -RATE, "w2_slot")
+
+        w1_rows = w1.rearrange("(p j) n -> p j n", j=4)
+        w1a_raw = keep.tile([P, 4, P], F32, name="w1a_raw", tag="w1a_slot", align_bytes=64)
+        x_sb = keep.tile([P, T], I32, name="x_sb", tag="x_slot", align_bytes=64)
+        w1b_raw = keep.tile([P, 4, P], F32, name="w1b_raw", tag="w1b_slot", align_bytes=64)
+        w2_raw = keep.tile([P, 4, N], F32, name="w2_raw", tag="w2_slot", align_bytes=64)
+        nc.sync.dma_start(offs_sb[:], offs)
+        nc.sync.dma_start(w1a_raw[:], w1_rows[:, :, 0:P])
+        for q in range(4):
+            nc.sync.dma_start(xs_sb[32 * q : 32 * q + 4, :].bitcast(I32), x_scales[0, 4 * q : 4 * q + 4, :].bitcast(I32))
+        nc.sync.dma_start(x_sb[:], x_words[0].rearrange("p n t -> p (n t)").bitcast(I32))
+        nc.sync.dma_start(w1b_raw[:], w1_rows[:, :, P:N])
+        nc.sync.dma_start(w2_raw[:], w2.rearrange("(p j) n -> p j n", j=4))
+        nc.sync.dma_start(oth_sb[:], oth)
+
+        ident = keep.tile([P, P], F32, name="ident")
+        make_identity(nc, ident[:])
+
+        raw = [[w1a_raw[:], w1b_raw[:]], [w2_raw[:, :, 0:P], w2_raw[:, :, P:N]]]
+        w_bf = [[keep.tile([P, P, 4], BF16, name=f"w_bf{i}{t}", align_bytes=64) for t in range(2)] for i in range(2)]
+        w_codes = [[keep.tile([P, P], U32, name=f"w_codes{i}{t}", align_bytes=64) for t in range(2)] for i in range(2)]
+        w_scales = [[keep.tile([P, P], U8, name=f"w_scales{i}{t}", align_bytes=64) for t in range(2)] for i in range(2)]
+        xg = [keep.tile([P, PIECE], U32, name=f"xg{g}", align_bytes=64) for g in range(4)]
+        xsg = [keep.tile([P, HALF], U8, name=f"xsg{h}", align_bytes=64) for h in range(2)]
+
+        def cols(h):
+            return slice(h * HALF, (h + 1) * HALF)
+
+        def entries(lst, a, b):
+            return lst[:, a // 16 : b // 16]
+
+        def views(i, t):
+            return w_bf[i][t][:].rearrange("p (c i) t -> p c t i", i=4), raw[i][t].rearrange("p t (c i) -> p c t i", i=4)
+
+        def quantize(i, t):
+            nc.vector.quantize_mx(out=w_codes[i][t][:].bitcast(FP8X4), scales=w_scales[i][t][:], in_=w_bf[i][t][:].rearrange("p n t -> p (n t)"))
+
+        nc.scalar.copy(*views(0, 0))
+        nc.scalar.copy(*views(0, 1))
+        nc.vector.tensor_copy(xsg[0][:], xs_sb[:].indirect(entries(offs_sb, 0, HALF)))
+        quantize(0, 0)
+        nc.vector.tensor_copy(xsg[1][:], xs_sb[:].indirect(entries(offs_sb, HALF, S)))
+        for g in range(4):
+            nc.vector.tensor_copy(xg[g][:], x_sb[:].bitcast(U32).indirect(entries(offs_sb, g * PIECE, (g + 1) * PIECE)))
+            if g == 0:
+                quantize(0, 1)
+        nc.vector.tensor_copy(*views(1, 0))
+        nc.vector.tensor_copy(*views(1, 1))
+        quantize(1, 0)
+        quantize(1, 1)
+
+        ey = [keep.tile([P, S], F32, name=f"ey{t}") for t in range(2)]
+        ez = [keep.tile([P, S], F32, name=f"ez{t}") for t in range(2)]
+
+        def product(i, t, h):
+            acc = psum.tile([P, HALF], F32, name=f"acc{i}{t}{h}", tag=f"bank{4 * i + 2 * t + h}")
+            for u in range(2):
+                c = slice(u * PIECE, (u + 1) * PIECE)
+                nc.tensor.matmul_mx(out=acc[:, c], lhsT=w_codes[i][t][:].bitcast(FP8X4), lhsT_scale=w_scales[i][t][:],
+                                    rhs=xg[2 * h + u][:].bitcast(FP8X4), rhs_scale=xsg[h][:, c], start=True, stop=True)
+            return acc
+
+        for h in range(2):
+            for t in range(2):
+                nc.scalar.activation(ey[t][:, cols(h)], product(0, t, h)[:], ACT.Exp)
+        for t in range(2):
+            for h in range(2):
+                nc.scalar.activation(ez[t][:, cols(h)], product(1, t, h)[:], ACT.Exp)
+                nc.vector.tensor_tensor(ey[t][:, cols(h)], ey[t][:, cols(h)], ez[t][:, cols(h)], ALU.max)
+
+        reg = [ez[1], ez[0]]
+        for t in range(2):
+            nc.scalar.activation(reg[t][:], ey[t][:], ACT.Ln, bias=floor_col[:], scale=2.0 ** -SHIFT_BITS)
+        uni = [keep.tile([P, S], F32, name=f"uni{t}") for t in range(2)]
+        cuts = [[0, 512, 1024], [0, 512, 768, 1024]]
+        for t in range(2):
+            for a, b in zip(cuts[t], cuts[t][1:]):
+                nc.vector.tensor_copy(uni[t][:, a:b], reg[t][:].indirect(entries(oth_sb, a, b)))
+                nc.vector.tensor_tensor(uni[t][:, a:b], uni[t][:, a:b], reg[t][:, a:b], ALU.max)
+
+        inv = [ey[1], ey[0]]
+        iu = [keep.tile([P, S], F32, name=f"iu{t}") for t in range(2)]
+        tot = psum.tile([P, N], F32, name="tot", tag="bank0")
+        tu = psum.tile([P, N], F32, name="tu", tag="bank1")
+
+        def weigh(dest, src, a, b):
+            nc.scalar.activation(dest[:].rearrange("p (a b v) -> p a v b", a=2, b=4)[:, :, a // D : b // D, :],
+                                 src[:].rearrange("p (v a b) -> p a v b", a=2, b=4)[:, :, a // D : b // D, :], ACT.Exp, scale=rate_col[:])
+
+        def group_sum(dest, src, t):
+            for dd in range(D):
+                nc.tensor.matmul(dest[:, t * P : (t + 1) * P], src[:, dd * V : (dd + 1) * V], ident[:], is_transpose=True, start=dd == 0, stop=dd == D - 1)
+
+        for t in range(2):
+            weigh(inv[t], reg[t], 0, S)
+            group_sum(tot, inv[t], t)
+        weigh(iu[0], uni[0], 0, S)
+        group_sum(tu, iu[0], 0)
+        for a, b in zip(cuts[1], cuts[1][1:]):
+            weigh(iu[1], uni[1], a, b)
+        group_sum(tu, iu[1], 1)
+        alpha_col = keep.tile([P, 1], F32, name="alpha_col", tag="w1a_slot", align_bytes=64)
+        est_col = keep.tile([P, 1], F32, name="est_col")
+        nc.sync.dma_start(alpha_col[:], alpha[0:1, :].rearrange("o v -> v o"))
+        nc.vector.tensor_scalar_mul(est_col[:], alpha_col[:], -0.02 * math.exp(RATE * SHIFT_BITS * math.log(2.0)))
+        rec = keep.tile([P, N], F32, name="rec")
+        nest = keep.tile([P, N], F32, name="nest")
+        ratio = keep.tile([P, N], F32, name="ratio")
+        lnr = keep.tile([P, N], F32, name="lnr")
+        nc.vector.reciprocal(rec[:], tot[:])
+        nc.vector.tensor_tensor(ratio[:], tu[:], rec[:], ALU.mult)
+        nc.vector.tensor_scalar(nest[:], rec[:], est_col[:], shift_col[:], ALU.mult, ALU.add)
+        nc.scalar.activation(lnr[:], ratio[:], ACT.Ln, scale=2.0 ** RATIO_BITS)
+        for t in range(2):
+            m = slice(t * P, (t + 1) * P)
+            res = psum.tile([P, V], F32, name=f"res{t}", tag=f"bank{2 + t}")
+            nc.tensor.matmul(res[:], nest[:, m], ident[:], is_transpose=True, start=True, stop=False)
+            nc.tensor.matmul(res[:], lnr[:, m], ident[:], is_transpose=True, start=False, stop=True)
+            res_sb = keep.tile([P, V], F32, name=f"res_sb{t}")
+            if t == 0:
+                nc.vector.tensor_scalar_mul(res_sb[:], res[:], -1.0)
+                nc.sync.dma_start(out[m, :], res_sb[:])
+            else:
+                nc.scalar.activation(res_sb[:], res[:], ACT.Copy, scale=-1.0)
+                nc.scalar.dma_start(out[m, :], res_sb[:])

@@ -34,41 +34,34 @@ def tile_picked_yhll_union_p_kernel(tc, x_words, x_scales, w1, w2, alpha, offs, 
         oth_sb = keep.tile([P, S // 16], U16, name="oth_sb")
         xs_sb = keep.tile([P, T], U8, name="xs_sb", align_bytes=64)
 
-        def constant_column(name, value, slot):
-            unit = keep.tile([P, 1], F32, name=name + "_unit", tag=slot, align_bytes=64)
-            col = keep.tile([P, 1], F32, name=name)
-            nc.vector.memset(unit[:], 1.0)
-            nc.vector.tensor_scalar_mul(col[:], unit[:], value)
-            return col
+        nc.vector.memset(xs_sb[:, 0 : T // 2].bitcast(I32), 0)
+        nc.gpsimd.memset(xs_sb[:, T // 2 : T].bitcast(I32), 0)
 
-        nc.vector.memset(xs_sb[:].bitcast(I32), 0)
-        floor_col = constant_column("floor_col", 2.0 ** -SHIFT_BITS, "x_slot")
-        shift_col = constant_column("shift_col", -RATIO_BITS * math.log(2.0), "w1b_slot")
-        rate_col = constant_column("rate_col", -RATE, "w2_slot")
-
-        w1_rows = w1.rearrange("(p j) n -> p j n", j=4)
-        w1a_raw = keep.tile([P, 4, P], F32, name="w1a_raw", tag="w1a_slot", align_bytes=64)
-        x_sb = keep.tile([P, T], I32, name="x_sb", tag="x_slot", align_bytes=64)
-        w1b_raw = keep.tile([P, 4, P], F32, name="w1b_raw", tag="w1b_slot", align_bytes=64)
-        w2_raw = keep.tile([P, 4, N], F32, name="w2_raw", tag="w2_slot", align_bytes=64)
+        w1_raw = keep.tile([P, 4, N], F32, name="w1_raw", align_bytes=64)
+        x_sb = keep.tile([P, T], I32, name="x_sb", align_bytes=64)
+        w2_raw = keep.tile([P, 4, N], F32, name="w2_raw", align_bytes=64)
+        alpha_col = keep.tile([P, 1], F32, name="alpha_col")
         nc.sync.dma_start(offs_sb[:], offs)
-        nc.sync.dma_start(w1a_raw[:], w1_rows[:, :, 0:P])
+        nc.scalar.dma_start(alpha_col[:], alpha[0:1, :].rearrange("o v -> v o"))
         for q in range(4):
-            nc.sync.dma_start(xs_sb[32 * q : 32 * q + 4, :].bitcast(I32), x_scales[0, 4 * q : 4 * q + 4, :].bitcast(I32))
+            (nc.sync if q % 2 == 0 else nc.scalar).dma_start(xs_sb[32 * q : 32 * q + 4, :].bitcast(I32), x_scales[0, 4 * q : 4 * q + 4, :].bitcast(I32))
+        nc.sync.dma_start(w1_raw[:], w1.rearrange("(p j) n -> p j n", j=4))
         nc.sync.dma_start(x_sb[:], x_words[0].rearrange("p n t -> p (n t)").bitcast(I32))
-        nc.sync.dma_start(w1b_raw[:], w1_rows[:, :, P:N])
         nc.sync.dma_start(w2_raw[:], w2.rearrange("(p j) n -> p j n", j=4))
         nc.sync.dma_start(oth_sb[:], oth)
+
+        est_col = keep.tile([P, 1], F32, name="est_col")
+        nc.scalar.activation(est_col[:], alpha_col[:], ACT.Copy, scale=-0.02 * math.exp(RATE * SHIFT_BITS * math.log(2.0)))
 
         ident = keep.tile([P, P], F32, name="ident")
         make_identity(nc, ident[:])
 
-        raw = [[w1a_raw[:], w1b_raw[:]], [w2_raw[:, :, 0:P], w2_raw[:, :, P:N]]]
-        w_bf = [[keep.tile([P, P, 4], BF16, name=f"w_bf{i}{t}", align_bytes=64) for t in range(2)] for i in range(2)]
+        raw = [[w[:, :, 0:P], w[:, :, P:N]] for w in (w1_raw, w2_raw)]
+        w_bf = [[keep.tile([P, P, 4], BF16, name=f"w_bf{i}{t}", tag=f"w_bf{i}{t}", align_bytes=64) for t in range(2)] for i in range(2)]
         w_codes = [[keep.tile([P, P], U32, name=f"w_codes{i}{t}", align_bytes=64) for t in range(2)] for i in range(2)]
         w_scales = [[keep.tile([P, P], U8, name=f"w_scales{i}{t}", align_bytes=64) for t in range(2)] for i in range(2)]
-        xg = [keep.tile([P, PIECE], U32, name=f"xg{g}", align_bytes=64) for g in range(4)]
         xsg = [keep.tile([P, HALF], U8, name=f"xsg{h}", align_bytes=64) for h in range(2)]
+        xg = []
 
         def cols(h):
             return slice(h * HALF, (h + 1) * HALF)
@@ -82,42 +75,54 @@ def tile_picked_yhll_union_p_kernel(tc, x_words, x_scales, w1, w2, alpha, offs, 
         def quantize(i, t):
             nc.vector.quantize_mx(out=w_codes[i][t][:].bitcast(FP8X4), scales=w_scales[i][t][:], in_=w_bf[i][t][:].rearrange("p n t -> p (n t)"))
 
-        nc.scalar.copy(*views(0, 0))
-        nc.scalar.copy(*views(0, 1))
-        nc.vector.tensor_copy(xsg[0][:], xs_sb[:].indirect(entries(offs_sb, 0, HALF)))
-        quantize(0, 0)
-        nc.vector.tensor_copy(xsg[1][:], xs_sb[:].indirect(entries(offs_sb, HALF, S)))
-        for g in range(4):
+        def gather_words(g, slot):
+            xg.append(keep.tile([P, PIECE], U32, name=f"xg{g}", tag=slot, align_bytes=64))
             nc.vector.tensor_copy(xg[g][:], x_sb[:].bitcast(U32).indirect(entries(offs_sb, g * PIECE, (g + 1) * PIECE)))
-            if g == 0:
-                quantize(0, 1)
-        nc.vector.tensor_copy(*views(1, 0))
-        nc.vector.tensor_copy(*views(1, 1))
-        quantize(1, 0)
-        quantize(1, 1)
-
-        ey = [keep.tile([P, S], F32, name=f"ey{t}") for t in range(2)]
-        ez = [keep.tile([P, S], F32, name=f"ez{t}") for t in range(2)]
-
-        def product(i, t, h):
-            acc = psum.tile([P, HALF], F32, name=f"acc{i}{t}{h}", tag=f"bank{4 * i + 2 * t + h}")
-            for u in range(2):
-                c = slice(u * PIECE, (u + 1) * PIECE)
-                nc.tensor.matmul_mx(out=acc[:, c], lhsT=w_codes[i][t][:].bitcast(FP8X4), lhsT_scale=w_scales[i][t][:],
-                                    rhs=xg[2 * h + u][:].bitcast(FP8X4), rhs_scale=xsg[h][:, c], start=True, stop=True)
-            return acc
 
         for h in range(2):
+            nc.vector.tensor_copy(xsg[h][:], xs_sb[:].indirect(entries(offs_sb, h * HALF, (h + 1) * HALF)))
+        for t in range(2):
+            nc.scalar.copy(*views(0, t))
+            quantize(0, t)
+        for g in range(4):
+            gather_words(g, f"xg{g}")
+        for t in range(2):
+            nc.vector.tensor_copy(*views(1, t))
+            quantize(1, t)
+
+        ey = keep.tile([P, 2, S], F32, name="ey")
+        ez = [keep.tile([P, S], F32, name=f"ez{t}") for t in range(2)]
+
+        def product(acc, i, t, g):
+            h, u = divmod(g, 2)
+            nc.tensor.matmul_mx(out=acc, lhsT=w_codes[i][t][:].bitcast(FP8X4), lhsT_scale=w_scales[i][t][:],
+                                rhs=xg[g][:].bitcast(FP8X4), rhs_scale=xsg[h][:, u * PIECE : (u + 1) * PIECE], start=True, stop=True)
+
+        def exp_y(g):
+            acc = psum.tile([P, 2, PIECE], F32, name=f"y{g}", tag=f"bank{g}")
             for t in range(2):
-                nc.scalar.activation(ey[t][:, cols(h)], product(0, t, h)[:], ACT.Exp)
+                product(acc[:, t, :], 0, t, g)
+            nc.scalar.activation(ey[:, :, g * PIECE : (g + 1) * PIECE], acc[:], ACT.Exp)
+
+        def exp_z(t, h):
+            acc = psum.tile([P, 2, PIECE], F32, name=f"z{t}{h}", tag=f"bank{4 + 2 * t + h}")
+            for u in range(2):
+                product(acc[:, u, :], 1, t, 2 * h + u)
+            nc.scalar.activation(ez[t][:, cols(h)], acc[:].rearrange("p u c -> p (u c)"), ACT.Exp)
+
+        for g in range(4):
+            exp_y(g)
+        exp_z(0, 0)
+        exp_z(0, 1)
+        exp_z(1, 0)
+        exp_z(1, 1)
         for t in range(2):
             for h in range(2):
-                nc.scalar.activation(ez[t][:, cols(h)], product(1, t, h)[:], ACT.Exp)
-                nc.vector.tensor_tensor(ey[t][:, cols(h)], ey[t][:, cols(h)], ez[t][:, cols(h)], ALU.max)
+                nc.vector.tensor_tensor(ey[:, t, cols(h)], ey[:, t, cols(h)], ez[t][:, cols(h)], ALU.max)
 
         reg = [ez[1], ez[0]]
         for t in range(2):
-            nc.scalar.activation(reg[t][:], ey[t][:], ACT.Ln, bias=floor_col[:], scale=2.0 ** -SHIFT_BITS)
+            nc.scalar.activation(reg[t][:], ey[:, t, :], ACT.Ln, bias=2.0 ** -SHIFT_BITS, scale=2.0 ** -SHIFT_BITS)
         uni = [keep.tile([P, S], F32, name=f"uni{t}") for t in range(2)]
         cuts = [[0, 512, 1024], [0, 512, 768, 1024]]
         for t in range(2):
@@ -125,14 +130,14 @@ def tile_picked_yhll_union_p_kernel(tc, x_words, x_scales, w1, w2, alpha, offs, 
                 nc.vector.tensor_copy(uni[t][:, a:b], reg[t][:].indirect(entries(oth_sb, a, b)))
                 nc.vector.tensor_tensor(uni[t][:, a:b], uni[t][:, a:b], reg[t][:, a:b], ALU.max)
 
-        inv = [ey[1], ey[0]]
-        iu = [keep.tile([P, S], F32, name=f"iu{t}") for t in range(2)]
+        inv = [ey[:, 1, :], ey[:, 0, :]]
+        iu = [keep.tile([P, S], F32, name=f"iu{t}")[:] for t in range(2)]
         tot = psum.tile([P, N], F32, name="tot", tag="bank0")
         tu = psum.tile([P, N], F32, name="tu", tag="bank1")
 
         def weigh(dest, src, a, b):
-            nc.scalar.activation(dest[:].rearrange("p (a b v) -> p a v b", a=2, b=4)[:, :, a // D : b // D, :],
-                                 src[:].rearrange("p (v a b) -> p a v b", a=2, b=4)[:, :, a // D : b // D, :], ACT.Exp, scale=rate_col[:])
+            nc.scalar.activation(dest.rearrange("p (a b v) -> p a v b", a=2, b=4)[:, :, a // D : b // D, :],
+                                 src[:].rearrange("p (v a b) -> p a v b", a=2, b=4)[:, :, a // D : b // D, :], ACT.Exp, scale=-RATE)
 
         def group_sum(dest, src, t):
             for dd in range(D):
@@ -146,17 +151,13 @@ def tile_picked_yhll_union_p_kernel(tc, x_words, x_scales, w1, w2, alpha, offs, 
         for a, b in zip(cuts[1], cuts[1][1:]):
             weigh(iu[1], uni[1], a, b)
         group_sum(tu, iu[1], 1)
-        alpha_col = keep.tile([P, 1], F32, name="alpha_col", tag="w1a_slot", align_bytes=64)
-        est_col = keep.tile([P, 1], F32, name="est_col")
-        nc.sync.dma_start(alpha_col[:], alpha[0:1, :].rearrange("o v -> v o"))
-        nc.vector.tensor_scalar_mul(est_col[:], alpha_col[:], -0.02 * math.exp(RATE * SHIFT_BITS * math.log(2.0)))
         rec = keep.tile([P, N], F32, name="rec")
         nest = keep.tile([P, N], F32, name="nest")
         ratio = keep.tile([P, N], F32, name="ratio")
         lnr = keep.tile([P, N], F32, name="lnr")
         nc.vector.reciprocal(rec[:], tot[:])
         nc.vector.tensor_tensor(ratio[:], tu[:], rec[:], ALU.mult)
-        nc.vector.tensor_scalar(nest[:], rec[:], est_col[:], shift_col[:], ALU.mult, ALU.add)
+        nc.vector.tensor_scalar(nest[:], rec[:], est_col[:], -RATIO_BITS * math.log(2.0), ALU.mult, ALU.add)
         nc.scalar.activation(lnr[:], ratio[:], ACT.Ln, scale=2.0 ** RATIO_BITS)
         for t in range(2):
             m = slice(t * P, (t + 1) * P)

import math
from contextlib import ExitStack

import concourse.mybir as mybir
from concourse.masks import make_identity

F32 = mybir.dt.float32
BF16 = mybir.dt.bfloat16
I32 = mybir.dt.int32
U32 = mybir.dt.uint32
U16 = mybir.dt.uint16
U8 = mybir.dt.uint8
FP8X4 = mybir.dt.float8_e4m3fn_x4
ALU = mybir.AluOpType
ACT = mybir.ActivationFunctionType

P = 128
K, T, S, D, N, V = 512, 2048, 1024, 8, 256, 128
HALF = 512
PIECE = 256
FLOPS = 2 * 2 * K * N * S
RATE = 0.693147
SHIFT_BITS = 64
RATIO_BITS = 28


def tile_picked_yhll_union_p_kernel(tc, x_words, x_scales, w1, w2, alpha, offs, oth, out):
    nc = tc.nc
    with ExitStack() as ctx:
        keep = ctx.enter_context(tc.tile_pool(name="keep", bufs=1))
        psum = ctx.enter_context(tc.psum_pool(name="psum", bufs=1))

        offs_sb = keep.tile([P, S // 16], U16, name="offs_sb")
        oth_sb = keep.tile([P, S // 16], U16, name="oth_sb")
        xs_sb = keep.tile([P, T], U8, name="xs_sb", align_bytes=64)

        nc.vector.memset(xs_sb[:, 0 : T // 2].bitcast(I32), 0)
        nc.gpsimd.memset(xs_sb[:, T // 2 : T].bitcast(I32), 0)

        w1_raw = keep.tile([P, 4, N], F32, name="w1_raw", align_bytes=64)
        x_sb = keep.tile([P, T], I32, name="x_sb", align_bytes=64)
        w2_raw = keep.tile([P, 4, N], F32, name="w2_raw", align_bytes=64)
        alpha_col = keep.tile([P, 1], F32, name="alpha_col")
        nc.sync.dma_start(offs_sb[:], offs)
        nc.scalar.dma_start(alpha_col[:], alpha[0:1, :].rearrange("o v -> v o"))
        for q in range(4):
            (nc.sync if q % 2 == 0 else nc.scalar).dma_start(xs_sb[32 * q : 32 * q + 4, :].bitcast(I32), x_scales[0, 4 * q : 4 * q + 4, :].bitcast(I32))
        nc.sync.dma_start(w1_raw[:], w1.rearrange("(p j) n -> p j n", j=4))
        nc.sync.dma_start(x_sb[:], x_words[0].rearrange("p n t -> p (n t)").bitcast(I32))
        nc.sync.dma_start(w2_raw[:], w2.rearrange("(p j) n -> p j n", j=4))
        nc.sync.dma_start(oth_sb[:], oth)

        est_col = keep.tile([P, 1], F32, name="est_col")
        nc.scalar.activation(est_col[:], alpha_col[:], ACT.Copy, scale=-0.02 * math.exp(RATE * SHIFT_BITS * math.log(2.0)))

        ident = keep.tile([P, P], F32, name="ident")
        make_identity(nc, ident[:])

        raw = [[w[:, :, 0:P], w[:, :, P:N]] for w in (w1_raw, w2_raw)]
        w_bf = [[keep.tile([P, P, 4], BF16, name=f"w_bf{i}{t}", tag=f"w_bf{i}{t}", align_bytes=64) for t in range(2)] for i in range(2)]
        w_codes = [[keep.tile([P, P], U32, name=f"w_codes{i}{t}", align_bytes=64) for t in range(2)] for i in range(2)]
        w_scales = [[keep.tile([P, P], U8, name=f"w_scales{i}{t}", align_bytes=64) for t in range(2)] for i in range(2)]
        xsg = [keep.tile([P, HALF], U8, name=f"xsg{h}", align_bytes=64) for h in range(2)]
        xg = []

        def cols(h):
            return slice(h * HALF, (h + 1) * HALF)

        def entries(lst, a, b):
            return lst[:, a // 16 : b // 16]

        def views(i, t):
            return w_bf[i][t][:].rearrange("p (c i) t -> p c t i", i=4), raw[i][t].rearrange("p t (c i) -> p c t i", i=4)

        def quantize(i, t):
            nc.vector.quantize_mx(out=w_codes[i][t][:].bitcast(FP8X4), scales=w_scales[i][t][:], in_=w_bf[i][t][:].rearrange("p n t -> p (n t)"))

        def gather_words(g, slot):
            xg.append(keep.tile([P, PIECE], U32, name=f"xg{g}", tag=slot, align_bytes=64))
            nc.vector.tensor_copy(xg[g][:], x_sb[:].bitcast(U32).indirect(entries(offs_sb, g * PIECE, (g + 1) * PIECE)))

        for h in range(2):
            nc.vector.tensor_copy(xsg[h][:], xs_sb[:].indirect(entries(offs_sb, h * HALF, (h + 1) * HALF)))
        for t in range(2):
            nc.scalar.copy(*views(0, t))
            quantize(0, t)
        for g in range(4):
            gather_words(g, f"xg{g}")
        for t in range(2):
            nc.vector.tensor_copy(*views(1, t))
            quantize(1, t)

        ey = keep.tile([P, 2, S], F32, name="ey")
        ez = [keep.tile([P, S], F32, name=f"ez{t}") for t in range(2)]

        def product(acc, i, t, g):
            h, u = divmod(g, 2)
            nc.tensor.matmul_mx(out=acc, lhsT=w_codes[i][t][:].bitcast(FP8X4), lhsT_scale=w_scales[i][t][:],
                                rhs=xg[g][:].bitcast(FP8X4), rhs_scale=xsg[h][:, u * PIECE : (u + 1) * PIECE], start=True, stop=True)

        def exp_y(g):
            acc = psum.tile([P, 2, PIECE], F32, name=f"y{g}", tag=f"bank{g}")
            for t in range(2):
                product(acc[:, t, :], 0, t, g)
            nc.scalar.activation(ey[:, :, g * PIECE : (g + 1) * PIECE], acc[:], ACT.Exp)

        def exp_z(t, h):
            acc = psum.tile([P, 2, PIECE], F32, name=f"z{t}{h}", tag=f"bank{4 + 2 * t + h}")
            for u in range(2):
                product(acc[:, u, :], 1, t, 2 * h + u)
            nc.scalar.activation(ez[t][:, cols(h)], acc[:].rearrange("p u c -> p (u c)"), ACT.Exp)

        for g in range(4):
            exp_y(g)
        exp_z(0, 0)
        exp_z(0, 1)
        exp_z(1, 0)
        exp_z(1, 1)
        for t in range(2):
            for h in range(2):
                nc.vector.tensor_tensor(ey[:, t, cols(h)], ey[:, t, cols(h)], ez[t][:, cols(h)], ALU.max)

        reg = [ez[1], ez[0]]
        for t in range(2):
            nc.scalar.activation(reg[t][:], ey[:, t, :], ACT.Ln, bias=2.0 ** -SHIFT_BITS, scale=2.0 ** -SHIFT_BITS)
        uni = [keep.tile([P, S], F32, name=f"uni{t}") for t in range(2)]
        cuts = [[0, 512, 1024], [0, 512, 768, 1024]]
        for t in range(2):
            for a, b in zip(cuts[t], cuts[t][1:]):
                nc.vector.tensor_copy(uni[t][:, a:b], reg[t][:].indirect(entries(oth_sb, a, b)))
                nc.vector.tensor_tensor(uni[t][:, a:b], uni[t][:, a:b], reg[t][:, a:b], ALU.max)

        inv = [ey[:, 1, :], ey[:, 0, :]]
        iu = [keep.tile([P, S], F32, name=f"iu{t}")[:] for t in range(2)]
        tot = psum.tile([P, N], F32, name="tot", tag="bank0")
        tu = psum.tile([P, N], F32, name="tu", tag="bank1")

        def weigh(dest, src, a, b):
            nc.scalar.activation(dest.rearrange("p (a b v) -> p a v b", a=2, b=4)[:, :, a // D : b // D, :],
                                 src[:].rearrange("p (v a b) -> p a v b", a=2, b=4)[:, :, a // D : b // D, :], ACT.Exp, scale=-RATE)

        def group_sum(dest, src, t):
            for dd in range(D):
                nc.tensor.matmul(dest[:, t * P : (t + 1) * P], src[:, dd * V : (dd + 1) * V], ident[:], is_transpose=True, start=dd == 0, stop=dd == D - 1)

        for t in range(2):
            weigh(inv[t], reg[t], 0, S)
            group_sum(tot, inv[t], t)
        weigh(iu[0], uni[0], 0, S)
        group_sum(tu, iu[0], 0)
        for a, b in zip(cuts[1], cuts[1][1:]):
            weigh(iu[1], uni[1], a, b)
        group_sum(tu, iu[1], 1)
        rec = keep.tile([P, N], F32, name="rec")
        nest = keep.tile([P, N], F32, name="nest")
        ratio = keep.tile([P, N], F32, name="ratio")
        lnr = keep.tile([P, N], F32, name="lnr")
        nc.vector.reciprocal(rec[:], tot[:])
        nc.vector.tensor_tensor(ratio[:], tu[:], rec[:], ALU.mult)
        nc.vector.tensor_scalar(nest[:], rec[:], est_col[:], -RATIO_BITS * math.log(2.0), ALU.mult, ALU.add)
        nc.scalar.activation(lnr[:], ratio[:], ACT.Ln, scale=2.0 ** RATIO_BITS)
        for t in range(2):
            m = slice(t * P, (t + 1) * P)
            res = psum.tile([P, V], F32, name=f"res{t}", tag=f"bank{2 + t}")
            nc.tensor.matmul(res[:], nest[:, m], ident[:], is_transpose=True, start=True, stop=False)
            nc.tensor.matmul(res[:], lnr[:, m], ident[:], is_transpose=True, start=False, stop=True)
            res_sb = keep.tile([P, V], F32, name=f"res_sb{t}")
            if t == 0:
                nc.vector.tensor_scalar_mul(res_sb[:], res[:], -1.0)
                nc.sync.dma_start(out[m, :], res_sb[:])
            else:
                nc.scalar.activation(res_sb[:], res[:], ACT.Copy, scale=-1.0)
                nc.scalar.dma_start(out[m, :], res_sb[:])
